import numpy as np
import ml_dtypes


def mxq(x, axis, fmt="e4m3"):
    dtype, down = {"e4m3": (ml_dtypes.float8_e4m3fn, 7), "e5m2": (ml_dtypes.float8_e5m2, 14)}[fmt]
    v = np.moveaxis(np.asarray(x, np.float32).astype(ml_dtypes.bfloat16).astype(np.float64), axis, -1)
    blocks = v.reshape(v.shape[:-1] + (-1, 32))
    amax = np.abs(blocks).max(-1, keepdims=True)
    byte = np.maximum(np.where(amax > 0, np.frexp(amax)[1] - 1 + 127, 0) - down, 1)
    scale = np.exp2(byte - 127.0)
    codes = (blocks / scale).astype(np.float32).astype(dtype).astype(np.float64)
    return np.moveaxis((codes * scale).reshape(v.shape), -1, axis)


WIDE = False


def mx_kscale(k):
    if not WIDE:
        return np.ones(k)
    levels = np.array([10, -10, 5, -5, 0])
    if k % 512:
        return np.exp2(np.random.permutation(np.resize(levels, k // 32))).repeat(32)
    a = np.empty((k // 512, 16))
    for p in range(k // 512):
        a[p, :8] = np.random.permutation(np.resize(levels, 8))
        for g in range(8):
            far = levels[np.abs(levels - a[p, g]) >= 10]
            a[p, g + 8] = far[np.random.randint(len(far))]
    return np.exp2(a.ravel()).repeat(32)


BF16 = ml_dtypes.bfloat16


def bf(x):
    return np.asarray(x, np.float32).astype(BF16)


def f64(x):
    return np.asarray(x).astype(np.float64)


E2M1 = np.array([0.0, 0.5, 1.0, 1.5, 2.0, 3.0, 4.0, 6.0, -0.0, -0.5, -1.0, -1.5, -2.0, -3.0, -4.0, -6.0])


def pack_weight(w, fmt):
    k, n = w.shape
    w = f64(bf(w)).reshape(k // 32, 32, n)
    amax = np.abs(w).max(1)
    if fmt == "e4m3":
        byte = np.frexp(amax)[1] - 1 + 127 - 7
    else:
        mant, ex = np.frexp(amax / 6.0)
        byte = np.where(mant > 0.5, ex, ex - 1) + 127
    byte = np.clip(np.where(amax > 0, byte, 1), 1, 254)
    scaled = (w * np.exp2(127.0 - byte)[:, None, :]).reshape(k, n).astype(np.float32)
    by_word = np.ascontiguousarray(scaled.reshape(k // 512, 128, 4, n).transpose(0, 1, 3, 2))
    if fmt == "e4m3":
        words = by_word.astype(ml_dtypes.float8_e4m3fn).view(np.uint8)
    else:
        c = by_word.astype(ml_dtypes.float4_e2m1fn).view(np.uint8) & 0xF
        words = c[..., 0::2] | (c[..., 1::2] << 4)
    return np.ascontiguousarray(words), np.ascontiguousarray(byte.astype(np.uint8).reshape(k // 512, 16, n))


def unpack_weight(words, scales, fmt):
    g, p, n, _ = words.shape
    if fmt == "e4m3":
        vals = np.ascontiguousarray(words).view(ml_dtypes.float8_e4m3fn).astype(np.float64)
    else:
        nib = np.empty((g, p, n, 4), np.uint8)
        nib[..., 0::2] = words & 0xF
        nib[..., 1::2] = words >> 4
        vals = E2M1[nib]
    vals = vals * np.repeat(np.exp2(scales.astype(np.float64) - 127.0), 8, axis=1)[..., None]
    return vals.transpose(0, 1, 3, 2).reshape(g * 512, n)
def pack4(w):
    words, scales = pack_weight(w, "e2m1")
    return words.reshape(words.shape[0], 128, -1), scales


def unpack4(words, scales):
    return unpack_weight(words.reshape(words.shape[0], 128, -1, 2), scales, "e2m1")


G, M, N = 4, 1024, 512

DIAG = 0.5


def setup_inputs():
    s = mx_kscale(N)
    t = mx_kscale(M)
    x = np.random.standard_normal((G, M, N)) * s * t[:, None]
    c = np.random.standard_normal((G, M, N)) * t[:, None]
    b = np.random.standard_normal((G * N, N)) / np.sqrt(N) - DIAG * np.tile(np.eye(N), (G, 1))
    b_words, b_scales = pack4(b / np.tile(s, G)[:, None])
    v = np.random.standard_normal((G * M, M)) / np.sqrt(M) + DIAG * np.tile(np.eye(M), (G, 1))
    v_words, v_scales = pack4(v / np.tile(t, G)[:, None])
    return {"x": bf(x), "c": bf(c),
            "b_words": b_words, "b_scales": b_scales,
            "v_words": v_words, "v_scales": v_scales}


def reference(x, c, b_words, b_scales, v_words, v_scales):
    b = unpack4(b_words, b_scales).reshape(G, N, N)
    v = unpack4(v_words, v_scales).reshape(G, M, M)
    xb = mxq(f64(x), 2, "e4m3") @ b
    r = f64(c) - xb
    return v.swapaxes(1, 2) @ mxq(r, 1, "e4m3")

@@ -1,0 +1,210 @@
+from contextlib import ExitStack
+
+import concourse.mybir as mybir
+from concourse.masks import make_identity
+
+G, M, N = 4, 1024, 512
+FLOPS = 2 * G * (M * N * N + M * M * N)
+
+F32 = mybir.dt.float32
+BF16 = mybir.dt.bfloat16
+I32 = mybir.dt.int32
+U32 = mybir.dt.uint32
+U8 = mybir.dt.uint8
+FP8X4 = mybir.dt.float8_e4m3fn_x4
+FP4X4 = mybir.dt.float4_e2m1fn_x4
+
+P = 128
+PACK = 4
+K_PASS = P * PACK
+HALVES = G * M // K_PASS
+CHUNK = 128
+CHUNKS = N // CHUNK
+ROW_TILES = M // P
+RUN = 4
+LAG = 10
+
+
+def tile_adi_half_step_s14_kernel(tc, x, c, b_words, b_scales, v_words, v_scales, out):
+    nc = tc.nc
+    with ExitStack() as ctx:
+        keep = ctx.enter_context(tc.tile_pool(name="keep", bufs=1))
+        work = ctx.enter_context(tc.tile_pool(name="work", bufs=4))
+        psum = ctx.enter_context(tc.psum_pool(name="psum", bufs=2))
+        ctx.enter_context(tc.manual_schedule())
+
+        ident = keep.tile([P, P], F32, name="ident")
+        make_identity(nc, ident[:])
+
+        def scale_tile(passes, width, name):
+            tile = keep.tile([P, passes, width], U8, name=name, align_bytes=64)
+            nc.vector.memset(tile[:].bitcast(I32), 0)
+            return tile
+
+        def load_scales(tile, rows):
+            by_r = rows.rearrange("g (q r) n -> r q g n", r=4)
+            for r in range(4):
+                nc.sync.dma_start(out=tile[r:P:32, :, :].bitcast(I32), in_=by_r[r].bitcast(I32))
+
+        def load_words(words, name):
+            tile = keep.tile([P, words.shape[0], words.shape[2]], U8, name=name, align_bytes=64)
+            nc.sync.dma_start(out=tile[:].bitcast(I32), in_=words.rearrange("g p n -> p g n").bitcast(I32))
+            return tile
+
+        def load_rows(src, h, slots, name):
+            rows = src[h // 2, (h % 2) * K_PASS:(h % 2 + 1) * K_PASS, :].rearrange("(p t) n -> p t n", t=PACK)
+            tile = keep.tile([P, slots.stop - slots.start, N], BF16, name=name, align_bytes=64)
+            nc.sync.dma_start(out=tile[:], in_=rows[:, slots, :])
+            return tile
+
+        b_sc = scale_tile(G, N, "b_sc")
+        v_sc_first = scale_tile(2, M, "v_sc_first")
+        v_sc_rest = scale_tile(2 * (G - 1), M, "v_sc_rest")
+
+        x_pairs = {}
+        c_rows = {}
+        v_w = {}
+
+        def load_x(h):
+            tile = load_rows(x, h, slice(0, PACK), "x%d" % h)
+            x_pairs[h, 0] = tile[:, 0:2, :]
+            x_pairs[h, 1] = tile[:, 2:4, :]
+
+        def load_c(h):
+            c_rows[h] = load_rows(c, h, slice(0, PACK), "c%d" % h)
+
+        def load_v(e):
+            v_w[e] = load_words(v_words[2 * e:2 * e + 2], "v_w%d" % e)
+
+        x_pairs[0, 0] = load_rows(x, 0, slice(0, 2), "x0a")[:]
+        x_pairs[0, 1] = load_rows(x, 0, slice(2, 4), "x0b")[:]
+        b_w_first = load_words(b_words[0:1], "b_w_first")
+        load_scales(b_sc, b_scales)
+        load_x(1)
+        load_c(0)
+        load_c(1)
+        load_x(2)
+        b_w_rest = load_words(b_words[1:G], "b_w_rest")
+        load_c(2)
+        load_v(0)
+        load_scales(v_sc_first, v_scales[0:2])
+        load_x(3)
+        load_c(3)
+        load_x(4)
+        load_v(1)
+        load_scales(v_sc_rest, v_scales[2:2 * G])
+        load_c(4)
+        load_x(5)
+        load_c(5)
+        load_x(6)
+        load_v(2)
+        load_c(6)
+        load_x(7)
+        load_c(7)
+        load_v(3)
+
+        x_grouped = {}
+        x_codes = {}
+        r_grouped = {}
+        r_codes = {}
+        results = {}
+
+        def transpose_x(h):
+            for pair in range(2):
+                words = x_pairs[h, pair].bitcast(F32)
+                bank = psum.tile([P, 2, 2, P], F32, name="t_bank", bufs=2)
+                for t in range(2):
+                    for u in range(2):
+                        nc.tensor.transpose(bank[:, t, u, :], words[:, t, u:N // 2:2], ident[:])
+                grouped = work.tile([P, 2 * P * PACK], BF16, name="x_grouped", align_bytes=64)
+                nc.scalar.copy(
+                    out=grouped[:].bitcast(F32).rearrange("p (t m u) -> p t m u", t=2, u=2),
+                    in_=bank[:].rearrange("p t u m -> p t m u"),
+                )
+                x_grouped[h, pair] = grouped
+
+        def quantize_x(h):
+            codes = work.tile([P, PACK * P], U32, name="x_codes", bufs=3, align_bytes=64)
+            scales = work.tile([P, PACK * P], U8, name="x_scales", bufs=3, align_bytes=64)
+            for pair in range(2):
+                cols = slice(pair * 2 * P, (pair + 1) * 2 * P)
+                nc.vector.quantize_mx(out=codes[:, cols].bitcast(FP8X4), scales=scales[:, cols], in_=x_grouped[h, pair][:])
+            x_codes[h] = (codes, scales)
+
+        def right_side(h, k):
+            e = h // 2
+            codes, scales = x_codes[h]
+            b_w = b_w_first[:, 0, :] if e == 0 else b_w_rest[:, e - 1, :]
+            cols = slice(k * CHUNK, (k + 1) * CHUNK)
+            bank = psum.tile([P, PACK, CHUNK], F32, name="xb_bank", bufs=3)
+            for t in range(PACK):
+                nc.tensor.matmul_mx(
+                    out=bank[:, t, :],
+                    lhsT=codes[:, t * P:(t + 1) * P].bitcast(FP8X4),
+                    lhsT_scale=scales[:, t * P:(t + 1) * P],
+                    rhs=b_w[:, 2 * cols.start:2 * cols.stop].bitcast(FP4X4),
+                    rhs_scale=b_sc[:, e, cols],
+                    start=True,
+                    stop=True,
+                )
+            if k == 0:
+                r_grouped[h] = work.tile([P, N, PACK], BF16, name="r_grouped", bufs=2, align_bytes=64)
+            nc.vector.tensor_tensor(
+                out=r_grouped[h][:, cols, :].rearrange("p (a i) t -> p a t i", i=RUN),
+                in0=c_rows[h][:, :, cols].rearrange("p t (a i) -> p a t i", i=RUN),
+                in1=bank[:].rearrange("p t (a i) -> p a t i", i=RUN),
+                op=mybir.AluOpType.subtract,
+            )
+
+        def quantize_r(h):
+            codes = work.tile([P, N], U32, name="r_codes", bufs=5, align_bytes=64)
+            scales = work.tile([P, N], U8, name="r_scales", bufs=5, align_bytes=64)
+            nc.vector.quantize_mx(
+                out=codes[:].bitcast(FP8X4), scales=scales[:], in_=r_grouped[h][:].rearrange("p n t -> p (n t)")
+            )
+            r_codes[h] = (codes, scales)
+
+        def solve(s):
+            e, j = divmod(s, ROW_TILES)
+            v_sc = v_sc_first if e == 0 else v_sc_rest[:, 2 * (e - 1):2 * e, :]
+            bank = psum.tile([P, N], F32, name="out_bank", bufs=3)
+            for g in range(2):
+                codes, scales = r_codes[2 * e + g]
+                nc.tensor.matmul_mx(
+                    out=bank[:],
+                    lhsT=v_w[e][:, g, 2 * j * P:2 * (j + 1) * P].bitcast(FP4X4),
+                    lhsT_scale=v_sc[:, g, j * P:(j + 1) * P],
+                    rhs=codes[:].bitcast(FP8X4),
+                    rhs_scale=scales[:],
+                    start=(g == 0),
+                    stop=(g == 1),
+                )
+            if j % 2 == 0:
+                results[s // 2] = work.tile([P, 2, N], F32, name="result", bufs=G * ROW_TILES // 2)
+            result = results[s // 2]
+            last = e == G - 1
+            if last and j % 2 == 0:
+                nc.vector.tensor_copy(out=result[:, j % 2, :], in_=bank[:])
+            else:
+                nc.scalar.copy(out=result[:, j % 2, :], in_=bank[:])
+            if last:
+                nc.sync.dma_start(out=out[e, j * P:(j + 1) * P, :], in_=result[:, j % 2, :])
+            elif j % 2 == 1:
+                nc.sync.dma_start(
+                    out=out[e, (j - 1) * P:(j + 1) * P, :].rearrange("(a p) n -> p a n", p=P), in_=result[:]
+                )
+
+        transpose_x(0)
+        quantize_x(0)
+        for h in range(HALVES):
+            if h + 1 < HALVES:
+                transpose_x(h + 1)
+            for k in range(CHUNKS):
+                right_side(h, k)
+                if CHUNKS * h + k >= LAG:
+                    solve(CHUNKS * h + k - LAG)
+            if h + 1 < HALVES:
+                quantize_x(h + 1)
+            quantize_r(h)
+        for s in range(HALVES * CHUNKS - LAG, G * ROW_TILES):
+            solve(s)

@@ -22,7 +22,8 @@ CHUNK = 128
 CHUNKS = N // CHUNK
 ROW_TILES = M // P
 RUN = 4
-LAG = 10
+LAG = 9
+SORT_FROM = 4
 
 
 def tile_adi_half_step_s14_kernel(tc, x, c, b_words, b_scales, v_words, v_scales, out):
@@ -51,11 +52,17 @@ def tile_adi_half_step_s14_kernel(tc, x, c, b_words, b_scales, v_words, v_scales
             nc.sync.dma_start(out=tile[:].bitcast(I32), in_=words.rearrange("g p n -> p g n").bitcast(I32))
             return tile
 
-        def load_rows(src, h, slots, name):
-            rows = src[h // 2, (h % 2) * K_PASS:(h % 2 + 1) * K_PASS, :].rearrange("(p t) n -> p t n", t=PACK)
-            tile = keep.tile([P, slots.stop - slots.start, N], BF16, name=name, align_bytes=64)
-            nc.sync.dma_start(out=tile[:], in_=rows[:, slots, :])
+        def load_halves(src, first, count, name):
+            rows = src.rearrange("e (g p t) n -> p (e g) t n", p=P, t=PACK)
+            tile = keep.tile([P, count, PACK, N], BF16, name=name, align_bytes=64)
+            nc.sync.dma_start(out=tile[:], in_=rows[:, first:first + count, :, :])
             return tile
+
+        def load_x_pair(h, pair):
+            rows = x.rearrange("e (g p t) n -> p (e g) t n", p=P, t=PACK)
+            tile = keep.tile([P, 2, N], BF16, name="x%d_%d" % (h, pair), align_bytes=64)
+            nc.sync.dma_start(out=tile[:], in_=rows[:, h, 2 * pair:2 * pair + 2, :])
+            x_pairs[h, pair] = tile[:]
 
         b_sc = scale_tile(G, N, "b_sc")
         v_sc_first = scale_tile(2, M, "v_sc_first")
@@ -65,57 +72,69 @@ def tile_adi_half_step_s14_kernel(tc, x, c, b_words, b_scales, v_words, v_scales
         c_rows = {}
         v_w = {}
 
-        def load_x(h):
-            tile = load_rows(x, h, slice(0, PACK), "x%d" % h)
-            x_pairs[h, 0] = tile[:, 0:2, :]
-            x_pairs[h, 1] = tile[:, 2:4, :]
+        def load_x(first, count=1):
+            tile = load_halves(x, first, count, "x%d" % first)
+            for i in range(count):
+                for pair in range(2):
+                    x_pairs[first + i, pair] = tile[:, i, 2 * pair:2 * pair + 2, :]
 
-        def load_c(h):
-            c_rows[h] = load_rows(c, h, slice(0, PACK), "c%d" % h)
+        def load_c(first, count=1):
+            tile = load_halves(c, first, count, "c%d" % first)
+            for i in range(count):
+                c_rows[first + i] = tile[:, i, :, :]
 
-        def load_v(e):
-            v_w[e] = load_words(v_words[2 * e:2 * e + 2], "v_w%d" % e)
+        def load_v(first, count=1):
+            tile = load_words(v_words[2 * first:2 * (first + count)], "v_w%d" % first)
+            for i in range(count):
+                v_w[first + i] = tile[:, 2 * i:2 * i + 2, :]
 
-        x_pairs[0, 0] = load_rows(x, 0, slice(0, 2), "x0a")[:]
-        x_pairs[0, 1] = load_rows(x, 0, slice(2, 4), "x0b")[:]
+        for h in range(2):
+            for pair in range(2):
+                load_x_pair(h, pair)
         b_w_first = load_words(b_words[0:1], "b_w_first")
         load_scales(b_sc, b_scales)
-        load_x(1)
         load_c(0)
-        load_c(1)
         load_x(2)
+        load_c(1)
+        load_x(3)
         b_w_rest = load_words(b_words[1:G], "b_w_rest")
         load_c(2)
         load_v(0)
         load_scales(v_sc_first, v_scales[0:2])
-        load_x(3)
-        load_c(3)
         load_x(4)
+        load_c(3)
+        load_x(5)
+        load_c(4)
         load_v(1)
         load_scales(v_sc_rest, v_scales[2:2 * G])
-        load_c(4)
-        load_x(5)
+        load_x(6, 2)
         load_c(5)
-        load_x(6)
-        load_v(2)
-        load_c(6)
-        load_x(7)
-        load_c(7)
-        load_v(3)
+        load_c(6, 2)
+        load_v(2, 2)
 
+        x_sorted = {}
         x_grouped = {}
         x_codes = {}
         r_grouped = {}
         r_codes = {}
         results = {}
 
+        def sort_x(h):
+            for pair in range(2):
+                tile = work.tile([P, 2, 2, P], F32, name="x_sorted")
+                nc.scalar.copy(out=tile[:], in_=x_pairs[h, pair].bitcast(F32).rearrange("p t (q u) -> p t u q", u=2))
+                x_sorted[h, pair] = tile
+
         def transpose_x(h):
             for pair in range(2):
-                words = x_pairs[h, pair].bitcast(F32)
+                if h >= SORT_FROM:
+                    words = x_sorted[h, pair][:]
+                else:
+                    words = x_pairs[h, pair].bitcast(F32).rearrange("p t (q u) -> p t u q", u=2)
                 bank = psum.tile([P, 2, 2, P], F32, name="t_bank", bufs=2)
                 for t in range(2):
                     for u in range(2):
-                        nc.tensor.transpose(bank[:, t, u, :], words[:, t, u:N // 2:2], ident[:])
+                        nc.tensor.transpose(bank[:, t, u, :], words[:, t, u, :], ident[:])
                 grouped = work.tile([P, 2 * P * PACK], BF16, name="x_grouped", align_bytes=64)
                 nc.scalar.copy(
                     out=grouped[:].bitcast(F32).rearrange("p (t m u) -> p t m u", t=2, u=2),
@@ -123,13 +142,14 @@ def tile_adi_half_step_s14_kernel(tc, x, c, b_words, b_scales, v_words, v_scales
                 )
                 x_grouped[h, pair] = grouped
 
-        def quantize_x(h):
-            codes = work.tile([P, PACK * P], U32, name="x_codes", bufs=3, align_bytes=64)
-            scales = work.tile([P, PACK * P], U8, name="x_scales", bufs=3, align_bytes=64)
-            for pair in range(2):
-                cols = slice(pair * 2 * P, (pair + 1) * 2 * P)
-                nc.vector.quantize_mx(out=codes[:, cols].bitcast(FP8X4), scales=scales[:, cols], in_=x_grouped[h, pair][:])
-            x_codes[h] = (codes, scales)
+        def quantize_x(h, pair):
+            if pair == 0:
+                codes = work.tile([P, PACK * P], U32, name="x_codes", bufs=3, align_bytes=64)
+                scales = work.tile([P, PACK * P], U8, name="x_scales", bufs=3, align_bytes=64)
+                x_codes[h] = (codes, scales)
+            codes, scales = x_codes[h]
+            cols = slice(pair * 2 * P, (pair + 1) * 2 * P)
+            nc.vector.quantize_mx(out=codes[:, cols].bitcast(FP8X4), scales=scales[:, cols], in_=x_grouped[h, pair][:])
 
         def right_side(h, k):
             e = h // 2
@@ -179,32 +199,38 @@ def tile_adi_half_step_s14_kernel(tc, x, c, b_words, b_scales, v_words, v_scales
                     start=(g == 0),
                     stop=(g == 1),
                 )
-            if j % 2 == 0:
-                results[s // 2] = work.tile([P, 2, N], F32, name="result", bufs=G * ROW_TILES // 2)
-            result = results[s // 2]
-            last = e == G - 1
-            if last and j % 2 == 0:
-                nc.vector.tensor_copy(out=result[:, j % 2, :], in_=bank[:])
+            size = 4 if s < 12 else 2 if s < 24 else 1
+            if s % 4 == 0:
+                results[s // 4] = work.tile([P, 4, N], F32, name="result", bufs=G * ROW_TILES // 4)
+            result = results[s // 4]
+            if e == G - 1 and j % 2 == 0:
+                nc.vector.tensor_copy(out=result[:, j % 4, :], in_=bank[:])
             else:
-                nc.scalar.copy(out=result[:, j % 2, :], in_=bank[:])
-            if last:
-                nc.sync.dma_start(out=out[e, j * P:(j + 1) * P, :], in_=result[:, j % 2, :])
-            elif j % 2 == 1:
+                nc.scalar.copy(out=result[:, j % 4, :], in_=bank[:])
+            if (j + 1) % size == 0:
+                first = j + 1 - size
                 nc.sync.dma_start(
-                    out=out[e, (j - 1) * P:(j + 1) * P, :].rearrange("(a p) n -> p a n", p=P), in_=result[:]
+                    out=out[e, first * P:(j + 1) * P, :].rearrange("(a p) n -> p a n", p=P),
+                    in_=result[:, first % 4:first % 4 + size, :],
                 )
 
-        transpose_x(0)
-        quantize_x(0)
+        for h in range(2):
+            transpose_x(h)
+            quantize_x(h, 0)
+            quantize_x(h, 1)
         for h in range(HALVES):
-            if h + 1 < HALVES:
+            ahead = 1 <= h < HALVES - 1
+            if ahead:
                 transpose_x(h + 1)
             for k in range(CHUNKS):
+                if k == 2 and SORT_FROM <= h + 2 < HALVES:
+                    sort_x(h + 2)
                 right_side(h, k)
+                if ahead and k in (1, 3):
+                    quantize_x(h + 1, k // 2)
+                if k == 3:
+                    quantize_r(h)
                 if CHUNKS * h + k >= LAG:
                     solve(CHUNKS * h + k - LAG)
-            if h + 1 < HALVES:
-                quantize_x(h + 1)
-            quantize_r(h)
         for s in range(HALVES * CHUNKS - LAG, G * ROW_TILES):
             solve(s)

@@ -23,7 +23,7 @@ CHUNKS = N // CHUNK
 ROW_TILES = M // P
 RUN = 4
 LAG = 9
-SORT_FROM = 4
+SORT_FROM = 2
 
 
 def tile_adi_half_step_s14_kernel(tc, x, c, b_words, b_scales, v_words, v_scales, out):
@@ -223,11 +223,11 @@ def tile_adi_half_step_s14_kernel(tc, x, c, b_words, b_scales, v_words, v_scales
             if ahead:
                 transpose_x(h + 1)
             for k in range(CHUNKS):
-                if k == 2 and SORT_FROM <= h + 2 < HALVES:
+                if k == 1 and SORT_FROM <= h + 2 < HALVES:
                     sort_x(h + 2)
                 right_side(h, k)
-                if ahead and k in (1, 3):
-                    quantize_x(h + 1, k // 2)
+                if ahead and k in (1, 2):
+                    quantize_x(h + 1, k - 1)
                 if k == 3:
                     quantize_r(h)
                 if CHUNKS * h + k >= LAG:

@@ -21,7 +21,7 @@ HALVES = G * M // K_PASS
 CHUNK = 128
 CHUNKS = N // CHUNK
 ROW_TILES = M // P
-RUN = 4
+RUN = 8
 LAG = 9
 SORT_FROM = 2
 

@@ -199,7 +199,7 @@ def tile_adi_half_step_s14_kernel(tc, x, c, b_words, b_scales, v_words, v_scales
                     start=(g == 0),
                     stop=(g == 1),
                 )
-            size = 4 if s < 12 else 2 if s < 24 else 1
+            size = 4 if e == 0 else 1 if e == G - 1 else 2
             if s % 4 == 0:
                 results[s // 4] = work.tile([P, 4, N], F32, name="result", bufs=G * ROW_TILES // 4)
             result = results[s // 4]
@@ -209,7 +209,8 @@ def tile_adi_half_step_s14_kernel(tc, x, c, b_words, b_scales, v_words, v_scales
                 nc.scalar.copy(out=result[:, j % 4, :], in_=bank[:])
             if (j + 1) % size == 0:
                 first = j + 1 - size
-                nc.sync.dma_start(
+                queue = nc.gpsimd if size == 2 and j % 4 == 1 and s < 20 else nc.sync
+                queue.dma_start(
                     out=out[e, first * P:(j + 1) * P, :].rearrange("(a p) n -> p a n", p=P),
                     in_=result[:, first % 4:first % 4 + size, :],
                 )

from contextlib import ExitStack

import concourse.mybir as mybir
from concourse.masks import make_identity

G, M, N = 4, 1024, 512
FLOPS = 2 * G * (M * N * N + M * M * N)

F32 = mybir.dt.float32
BF16 = mybir.dt.bfloat16
I32 = mybir.dt.int32
U32 = mybir.dt.uint32
U8 = mybir.dt.uint8
FP8X4 = mybir.dt.float8_e4m3fn_x4
FP4X4 = mybir.dt.float4_e2m1fn_x4

P = 128
PACK = 4
K_PASS = P * PACK
HALVES = G * M // K_PASS
CHUNK = 128
CHUNKS = N // CHUNK
ROW_TILES = M // P
RUN = 8
LAG = 9
SORT_FROM = 2


def tile_adi_half_step_s14_kernel(tc, x, c, b_words, b_scales, v_words, v_scales, out):
    nc = tc.nc
    with ExitStack() as ctx:
        keep = ctx.enter_context(tc.tile_pool(name="keep", bufs=1))
        work = ctx.enter_context(tc.tile_pool(name="work", bufs=4))
        psum = ctx.enter_context(tc.psum_pool(name="psum", bufs=2))
        ctx.enter_context(tc.manual_schedule())

        ident = keep.tile([P, P], F32, name="ident")
        make_identity(nc, ident[:])

        def scale_tile(passes, width, name):
            tile = keep.tile([P, passes, width], U8, name=name, align_bytes=64)
            nc.vector.memset(tile[:].bitcast(I32), 0)
            return tile

        def load_scales(tile, rows):
            by_r = rows.rearrange("g (q r) n -> r q g n", r=4)
            for r in range(4):
                nc.sync.dma_start(out=tile[r:P:32, :, :].bitcast(I32), in_=by_r[r].bitcast(I32))

        def load_words(words, name):
            tile = keep.tile([P, words.shape[0], words.shape[2]], U8, name=name, align_bytes=64)
            nc.sync.dma_start(out=tile[:].bitcast(I32), in_=words.rearrange("g p n -> p g n").bitcast(I32))
            return tile

        def load_halves(src, first, count, name):
            rows = src.rearrange("e (g p t) n -> p (e g) t n", p=P, t=PACK)
            tile = keep.tile([P, count, PACK, N], BF16, name=name, align_bytes=64)
            nc.sync.dma_start(out=tile[:], in_=rows[:, first:first + count, :, :])
            return tile

        def load_x_pair(h, pair):
            rows = x.rearrange("e (g p t) n -> p (e g) t n", p=P, t=PACK)
            tile = keep.tile([P, 2, N], BF16, name="x%d_%d" % (h, pair), align_bytes=64)
            nc.sync.dma_start(out=tile[:], in_=rows[:, h, 2 * pair:2 * pair + 2, :])
            x_pairs[h, pair] = tile[:]

        b_sc = scale_tile(G, N, "b_sc")
        v_sc_first = scale_tile(2, M, "v_sc_first")
        v_sc_rest = scale_tile(2 * (G - 1), M, "v_sc_rest")

        x_pairs = {}
        c_rows = {}
        v_w = {}

        def load_x(first, count=1):
            tile = load_halves(x, first, count, "x%d" % first)
            for i in range(count):
                for pair in range(2):
                    x_pairs[first + i, pair] = tile[:, i, 2 * pair:2 * pair + 2, :]

        def load_c(first, count=1):
            tile = load_halves(c, first, count, "c%d" % first)
            for i in range(count):
                c_rows[first + i] = tile[:, i, :, :]

        def load_v(first, count=1):
            tile = load_words(v_words[2 * first:2 * (first + count)], "v_w%d" % first)
            for i in range(count):
                v_w[first + i] = tile[:, 2 * i:2 * i + 2, :]

        for h in range(2):
            for pair in range(2):
                load_x_pair(h, pair)
        b_w_first = load_words(b_words[0:1], "b_w_first")
        load_scales(b_sc, b_scales)
        load_c(0)
        load_x(2)
        load_c(1)
        load_x(3)
        b_w_rest = load_words(b_words[1:G], "b_w_rest")
        load_c(2)
        load_v(0)
        load_scales(v_sc_first, v_scales[0:2])
        load_x(4)
        load_c(3)
        load_x(5)
        load_c(4)
        load_v(1)
        load_scales(v_sc_rest, v_scales[2:2 * G])
        load_x(6, 2)
        load_c(5)
        load_c(6, 2)
        load_v(2, 2)

        x_sorted = {}
        x_grouped = {}
        x_codes = {}
        r_grouped = {}
        r_codes = {}
        results = {}

        def sort_x(h):
            for pair in range(2):
                tile = work.tile([P, 2, 2, P], F32, name="x_sorted")
                nc.scalar.copy(out=tile[:], in_=x_pairs[h, pair].bitcast(F32).rearrange("p t (q u) -> p t u q", u=2))
                x_sorted[h, pair] = tile

        def transpose_x(h):
            for pair in range(2):
                if h >= SORT_FROM:
                    words = x_sorted[h, pair][:]
                else:
                    words = x_pairs[h, pair].bitcast(F32).rearrange("p t (q u) -> p t u q", u=2)
                bank = psum.tile([P, 2, 2, P], F32, name="t_bank", bufs=2)
                for t in range(2):
                    for u in range(2):
                        nc.tensor.transpose(bank[:, t, u, :], words[:, t, u, :], ident[:])
                grouped = work.tile([P, 2 * P * PACK], BF16, name="x_grouped", align_bytes=64)
                nc.scalar.copy(
                    out=grouped[:].bitcast(F32).rearrange("p (t m u) -> p t m u", t=2, u=2),
                    in_=bank[:].rearrange("p t u m -> p t m u"),
                )
                x_grouped[h, pair] = grouped

        def quantize_x(h, pair):
            if pair == 0:
                codes = work.tile([P, PACK * P], U32, name="x_codes", bufs=3, align_bytes=64)
                scales = work.tile([P, PACK * P], U8, name="x_scales", bufs=3, align_bytes=64)
                x_codes[h] = (codes, scales)
            codes, scales = x_codes[h]
            cols = slice(pair * 2 * P, (pair + 1) * 2 * P)
            nc.vector.quantize_mx(out=codes[:, cols].bitcast(FP8X4), scales=scales[:, cols], in_=x_grouped[h, pair][:])

        def right_side(h, k):
            e = h // 2
            codes, scales = x_codes[h]
            b_w = b_w_first[:, 0, :] if e == 0 else b_w_rest[:, e - 1, :]
            cols = slice(k * CHUNK, (k + 1) * CHUNK)
            bank = psum.tile([P, PACK, CHUNK], F32, name="xb_bank", bufs=3)
            for t in range(PACK):
                nc.tensor.matmul_mx(
                    out=bank[:, t, :],
                    lhsT=codes[:, t * P:(t + 1) * P].bitcast(FP8X4),
                    lhsT_scale=scales[:, t * P:(t + 1) * P],
                    rhs=b_w[:, 2 * cols.start:2 * cols.stop].bitcast(FP4X4),
                    rhs_scale=b_sc[:, e, cols],
                    start=True,
                    stop=True,
                )
            if k == 0:
                r_grouped[h] = work.tile([P, N, PACK], BF16, name="r_grouped", bufs=2, align_bytes=64)
            nc.vector.tensor_tensor(
                out=r_grouped[h][:, cols, :].rearrange("p (a i) t -> p a t i", i=RUN),
                in0=c_rows[h][:, :, cols].rearrange("p t (a i) -> p a t i", i=RUN),
                in1=bank[:].rearrange("p t (a i) -> p a t i", i=RUN),
                op=mybir.AluOpType.subtract,
            )

        def quantize_r(h):
            codes = work.tile([P, N], U32, name="r_codes", bufs=5, align_bytes=64)
            scales = work.tile([P, N], U8, name="r_scales", bufs=5, align_bytes=64)
            nc.vector.quantize_mx(
                out=codes[:].bitcast(FP8X4), scales=scales[:], in_=r_grouped[h][:].rearrange("p n t -> p (n t)")
            )
            r_codes[h] = (codes, scales)

        def solve(s):
            e, j = divmod(s, ROW_TILES)
            v_sc = v_sc_first if e == 0 else v_sc_rest[:, 2 * (e - 1):2 * e, :]
            bank = psum.tile([P, N], F32, name="out_bank", bufs=3)
            for g in range(2):
                codes, scales = r_codes[2 * e + g]
                nc.tensor.matmul_mx(
                    out=bank[:],
                    lhsT=v_w[e][:, g, 2 * j * P:2 * (j + 1) * P].bitcast(FP4X4),
                    lhsT_scale=v_sc[:, g, j * P:(j + 1) * P],
                    rhs=codes[:].bitcast(FP8X4),
                    rhs_scale=scales[:],
                    start=(g == 0),
                    stop=(g == 1),
                )
            size = 4 if e == 0 else 1 if e == G - 1 else 2
            if s % 4 == 0:
                results[s // 4] = work.tile([P, 4, N], F32, name="result", bufs=G * ROW_TILES // 4)
            result = results[s // 4]
            if e == G - 1 and j % 2 == 0:
                nc.vector.tensor_copy(out=result[:, j % 4, :], in_=bank[:])
            else:
                nc.scalar.copy(out=result[:, j % 4, :], in_=bank[:])
            if (j + 1) % size == 0:
                first = j + 1 - size
                queue = nc.gpsimd if size == 2 and j % 4 == 1 and s < 20 else nc.sync
                queue.dma_start(
                    out=out[e, first * P:(j + 1) * P, :].rearrange("(a p) n -> p a n", p=P),
                    in_=result[:, first % 4:first % 4 + size, :],
                )

        for h in range(2):
            transpose_x(h)
            quantize_x(h, 0)
            quantize_x(h, 1)
        for h in range(HALVES):
            ahead = 1 <= h < HALVES - 1
            if ahead:
                transpose_x(h + 1)
            for k in range(CHUNKS):
                if k == 1 and SORT_FROM <= h + 2 < HALVES:
                    sort_x(h + 2)
                right_side(h, k)
                if ahead and k in (1, 2):
                    quantize_x(h + 1, k - 1)
                if k == 3:
                    quantize_r(h)
                if CHUNKS * h + k >= LAG:
                    solve(CHUNKS * h + k - LAG)
        for s in range(HALVES * CHUNKS - LAG, G * ROW_TILES):
            solve(s)
